import numpy as np
import ml_dtypes


def mxq(x, axis, fmt="e4m3"):
    dtype, down = {"e4m3": (ml_dtypes.float8_e4m3fn, 7), "e5m2": (ml_dtypes.float8_e5m2, 14)}[fmt]
    v = np.moveaxis(np.asarray(x, np.float32).astype(ml_dtypes.bfloat16).astype(np.float64), axis, -1)
    blocks = v.reshape(v.shape[:-1] + (-1, 32))
    amax = np.abs(blocks).max(-1, keepdims=True)
    byte = np.maximum(np.where(amax > 0, np.frexp(amax)[1] - 1 + 127, 0) - down, 1)
    scale = np.exp2(byte - 127.0)
    codes = (blocks / scale).astype(np.float32).astype(dtype).astype(np.float64)
    return np.moveaxis((codes * scale).reshape(v.shape), -1, axis)


WIDE = False


def mx_kscale(k):
    if not WIDE:
        return np.ones(k)
    levels = np.array([10, -10, 5, -5, 0])
    if k % 512:
        return np.exp2(np.random.permutation(np.resize(levels, k // 32))).repeat(32)
    a = np.empty((k // 512, 16))
    for p in range(k // 512):
        a[p, :8] = np.random.permutation(np.resize(levels, 8))
        for g in range(8):
            far = levels[np.abs(levels - a[p, g]) >= 10]
            a[p, g + 8] = far[np.random.randint(len(far))]
    return np.exp2(a.ravel()).repeat(32)


BF16 = ml_dtypes.bfloat16


def bf(x):
    return np.asarray(x, np.float32).astype(BF16)


def f64(x):
    return np.asarray(x).astype(np.float64)

def planes(Y):
    n, m = Y.shape
    b = f64(bf(Y)).reshape(n // 32, 32, m)
    amax = np.abs(b).max(1)
    byte = np.clip(np.where(amax > 0, np.frexp(amax)[1] - 1 + 127 - 7, 1), 1, 254)
    codes = (b * np.exp2(127.0 - byte)[:, None, :]).reshape(n, m).astype(np.float32).astype(ml_dtypes.float8_e4m3fn).view(np.uint8)
    words = codes.reshape(n // 512, 128, 4, m).transpose(0, 1, 3, 2)
    return np.ascontiguousarray(words), np.ascontiguousarray(byte.astype(np.uint8).reshape(n // 512, 16, m))


B, S, D = 2, 512, 512


def setup_inputs():
    s, a = mx_kscale(D), mx_kscale(D)
    u, g = mx_kscale(D), mx_kscale(D)
    w = 1.0 / np.sqrt(D)
    return {
        "x": bf(np.random.standard_normal((B, S, D)) * s),
        "wq": bf(np.random.standard_normal((D, D)) * w / s[:, None] * a),
        "wk": bf(np.random.standard_normal((D, D)) * w / s[:, None] / a),
        "p": bf(np.random.standard_normal((S, D)) * u),
        "uq": bf(np.random.standard_normal((D, D)) * w / u[:, None] * g),
        "uk": bf(np.random.standard_normal((D, D)) * w / u[:, None] / g),
        "b": bf(np.random.standard_normal((S, S)) * 0.5),
    }


def softmax(v):
    ex = np.exp(v - v.max(axis=-1, keepdims=True))
    return ex / ex.sum(axis=-1, keepdims=True)


def core(x, wq, wk, p, uq, uk, b):
    seq_len = x.shape[1]
    dim = x.shape[2]

    xq = mxq(f64(x), 2, "e4m3")
    q = xq @ mxq(f64(wq), 0, "e4m3")
    k = xq @ mxq(f64(wk), 0, "e4m3")

    pq = mxq(f64(p), 1, "e4m3")
    r = pq @ mxq(f64(uq), 0, "e4m3")
    t = pq @ mxq(f64(uk), 0, "e4m3")

    c = mxq(q, 2, "e4m3") @ mxq(k, 2, "e4m3").transpose(0, 2, 1)

    e = mxq(r, 1, "e4m3") @ mxq(t, 1, "e4m3").T

    logits = (c + e[None, :, :]) / np.sqrt(2 * dim) + f64(b)[None, :, :]

    return seq_len * softmax(logits)


def reference(x, wq, wk, p, uq, uk, b):
    R_out = core(x, wq, wk, p, uq, uk, b)
    words, scales = planes(np.moveaxis(R_out, 1, 0).reshape(512, -1))
    return R_out, words, scales

from contextlib import ExitStack

import concourse.mybir as mybir
from concourse.masks import make_identity

F32 = mybir.dt.float32
BF16 = mybir.dt.bfloat16
U32 = mybir.dt.uint32
I32 = mybir.dt.int32
U8 = mybir.dt.uint8
FP8X4 = mybir.dt.float8_e4m3fn_x4
ALU = mybir.AluOpType
ACT = mybir.ActivationFunctionType
AX = mybir.AxisListType

P = 128
N = 512
FLOPS = 9 * 2 * 512 * 512 * 512
OF = {"r": ("uq", "p"), "t": ("uk", "p"), "q0": ("wq", "x0"), "k0": ("wk", "x0"), "q1": ("wq", "x1"), "k1": ("wk", "x1")}

PLAN = [
    ("load", "D", ("p", 0)),
    ("load", "D", ("uk", -1)),
    ("load", "D", ("p", 1)),
    ("load", "D", ("x0", 1)),
    ("load", "D", ("x0", 0)),
    ("load", "D", ("wk", -1)),
    ("load", "D", ("uq", -1)),
    ("load", "D", ("x1", 1)),
    ("load", "D", ("x1", 0)),
    ("load", "D", ("wq", -1)),
    ("load", "D", ("b", -1)),
    ("il", "S", ("uk", 3, 4)),
    ("il", "V", ("uk", 0, 3)),
    ("turn", "PE", ("p", 0)),
    ("untangle", "S", ("p", 0)),
    ("quant", "V", ("uk", 0, 4)),
    ("turn", "PE", ("p", 1)),
    ("untangle", "S", ("p", 1)),
    ("turn", "PE", ("x0", 1)),
    ("quant", "V", ("p", 0, 4)),
    ("il", "V", ("wk", 0, 4)),
    ("proj", "PE", ("t", 0)),
    ("turn", "PE", ("x0", 0)),
    ("untangle", "S", ("x0", 1)),
    ("proj", "PE", ("t", 3)),
    ("evac", "S", ("t", 0)),
    ("il", "V", ("uq", 2, 4)),
    ("proj", "PE", ("t", 2)),
    ("quant", "V", ("wk", 0, 4)),
    ("turn", "PE", ("x1", 1)),
    ("untangle", "S", ("x0", 0)),
    ("il", "S", ("uq", 0, 2)),
    ("evac", "S", ("t", 3)),
    ("quant", "V", ("x0", 0, 4)),
    ("proj", "PE", ("t", 1)),
    ("turn", "PE", ("x1", 0)),
    ("evac", "S", ("t", 2)),
    ("quant", "V", ("uq", 0, 4)),
    ("proj", "PE", ("k0", 1)),
    ("proj", "PE", ("k0", 2)),
    ("evac", "S", ("t", 1)),
    ("evac", "S", ("k0", 1)),
    ("evac", "S", ("k0", 2)),
    ("proj", "PE", ("k0", 0)),
    ("proj", "PE", ("r", 2)),
    ("evac", "S", ("k0", 0)),
    ("il", "V", ("wq", 0, 4)),
    ("proj", "PE", ("k0", 3)),
    ("quant", "V", ("wq", 0, 4)),
    ("evac", "V", ("r", 2)),
    ("proj", "PE", ("r", 0)),
    ("untangle", "S", ("x1", 1)),
    ("proj", "PE", ("q0", 0)),
    ("evac", "V", ("k0", 3)),
    ("quant", "V", ("k0", 2, 3)),
    ("untangle", "S", ("x1", 0)),
    ("evac", "S", ("r", 0)),
    ("evac", "S", ("q0", 0)),
    ("quant", "V", ("k0", 0, 1)),
    ("quant", "V", ("x1", 0, 4)),
    ("proj", "PE", ("r", 1)),
    ("proj", "PE", ("q0", 1)),
    ("evac", "S", ("q0", 1)),
    ("proj", "PE", ("r", 3)),
    ("evac", "V", ("r", 1)),
    ("evac", "S", ("r", 3)),
    ("quant", "V", ("k0", 1, 2)),
    ("quant", "V", ("r", 0, 1)),
    ("proj", "PE", ("k1", 3)),
    ("proj", "PE", ("k1", 0)),
    ("proj", "PE", ("q0", 2)),
    ("quant", "V", ("q0", 0, 2)),
    ("quant", "V", ("r", 1, 2)),
    ("quant", "V", ("t", 0, 4)),
    ("evac", "S", ("k1", 3)),
    ("quant", "V", ("k0", 3, 4)),
    ("proj", "PE", ("q0", 3)),
    ("evac", "S", ("k1", 0)),
    ("quant", "V", ("k1", 3, 4)),
    ("score", "PE", (0, 0)),
    ("quant", "V", ("k1", 0, 1)),
    ("evac", "S", ("q0", 3)),
    ("proj", "PE", ("k1", 2)),
    ("evac", "V", ("q0", 2)),
    ("quant", "V", ("r", 3, 4)),
    ("bias", "V", (0, 0)),
    ("score", "PE", (0, 1)),
    ("evac", "S", ("k1", 2)),
    ("peak", "V", (0, 0)),
    ("proj", "PE", ("k1", 1)),
    ("bias", "V", (0, 1)),
    ("quant", "V", ("q0", 2, 4)),
    ("peak", "V", (0, 1)),
    ("quant", "V", ("r", 2, 3)),
    ("proj", "PE", ("q1", 0)),
    ("exp", "S", (0, 0)),
    ("evac", "S", ("k1", 1)),
    ("proj", "PE", ("q1", 1)),
    ("evac", "S", ("q1", 0)),
    ("evac", "S", ("q1", 1)),
    ("score", "PE", (0, 3)),
    ("proj", "PE", ("q1", 3)),
    ("quant", "V", ("k1", 1, 3)),
    ("exp", "S", (0, 1)),
    ("score", "PE", (0, 2)),
    ("quant", "V", ("q1", 0, 1)),
    ("recip", "V", (0, 0)),
    ("bias", "V", (0, 3)),
    ("quant", "V", ("q1", 1, 2)),
    ("evac", "S", ("q1", 3)),
    ("peak", "V", (0, 3)),
    ("scale", "S", (0, 0)),
    ("bias", "V", (0, 2)),
    ("exp", "S", (0, 3)),
    ("proj", "PE", ("q1", 2)),
    ("quant", "V", ("q1", 3, 4)),
    ("evac", "S", ("q1", 2)),
    ("recip", "V", (0, 1)),
    ("score", "PE", (1, 1)),
    ("peak", "V", (0, 2)),
    ("exp", "S", (0, 2)),
    ("bias", "V", (1, 1)),
    ("scale", "S", (0, 1)),
    ("quant", "V", ("q1", 2, 3)),
    ("recip", "V", (0, 3)),
    ("peak", "V", (1, 1)),
    ("score", "PE", (1, 3)),
    ("recip", "V", (0, 2)),
    ("bias", "V", (1, 3)),
    ("scale", "S", (0, 3)),
    ("score", "PE", (1, 0)),
    ("bias", "V", (1, 0)),
    ("scale", "S", (0, 2)),
    ("exp", "S", (1, 1)),
    ("peak", "V", (1, 3)),
    ("inter", "S", (0, 3, 4)),
    ("score", "PE", (1, 2)),
    ("peak", "V", (1, 0)),
    ("bias", "V", (1, 2)),
    ("recip", "V", (1, 1)),
    ("exp", "S", (1, 3)),
    ("exp", "S", (1, 0)),
    ("recip", "V", (1, 3)),
    ("peak", "V", (1, 2)),
    ("inter", "V", (0, 0, 3)),
    ("scale", "S", (1, 1)),
    ("recip", "V", (1, 0)),
    ("exp", "S", (1, 2)),
    ("recip", "V", (1, 2)),
    ("scale", "V", (1, 3)),
    ("scale", "S", (1, 0)),
    ("scale", "V", (1, 2)),
    ("qout", "V", (0, 0, 4)),
    ("inter", "S", (1, 0, 1)),
    ("inter", "V", (1, 1, 3)),
    ("inter", "S", (1, 3, 4)),
    ("qout", "V", (1, 0, 4)),
]


def tile_tupeuntiedpositionalattentionmap_x1_kernel(tc, x, wq, wk, p, uq, uk, b, out_0, out_1, out_2):
    nc = tc.nc
    src = {"x0": x[0], "x1": x[1], "p": p, "wq": wq, "wk": wk, "uq": uq, "uk": uk, "b": b}
    words_out = out_1[0].rearrange("p m t -> p (m t)")

    with ExitStack() as ctx:
        keep = ctx.enter_context(tc.tile_pool(name="keep", bufs=1))
        pools = {"tp": ctx.enter_context(tc.psum_pool(name="tp", bufs=2)), "s1": ctx.enter_context(tc.psum_pool(name="s1", bufs=3)), "s2": ctx.enter_context(tc.psum_pool(name="s2", bufs=3))}
        ident = keep.tile([P, P], F32, name="ident", align_bytes=64)
        raw = {n: keep.tile([P, 4, N], BF16, name="raw_" + n, align_bytes=64) for n in src}
        grp = {n: keep.tile([P, N, 4], BF16, name="grp_" + n, align_bytes=64) for n in ("x0", "x1", "p", "wq", "wk", "uq", "uk", "r", "t", "q0", "k0", "q1", "k1", "o0", "o1")}
        codes = {n: keep.tile([P, N], U32, name="codes_" + n, align_bytes=64) for n in grp}
        scal = {n: keep.tile([P, N], U8, name="scal_" + n, align_bytes=64) for n in grp}
        logit = {n: keep.tile([P, 4, N], F32, name="logit%d" % n, align_bytes=64) for n in (0, 1)}
        expo = {n: keep.tile([P, 4, N], F32, name="expo%d" % n, align_bytes=64) for n in (0, 1)}
        outf = {n: keep.tile([P, 4, N], F32, name="outf%d" % n, align_bytes=64) for n in (0, 1)}
        peak = {n: keep.tile([P, 4], F32, name="peak%d" % n, align_bytes=64) for n in (0, 1)}
        tot = {n: keep.tile([P, 4], F32, name="tot%d" % n, align_bytes=64) for n in (0, 1)}
        inv = {n: keep.tile([P, 4], F32, name="inv%d" % n, align_bytes=64) for n in (0, 1)}
        warm = keep.tile([P, 2], F32, name="warm", align_bytes=64)
        bank = {}

        def flat(n):
            return grp[n][:].rearrange("p m t -> p (m t)")

        def fp8(n, c0, c1):
            return codes[n][:, c0:c1].bitcast(FP8X4)

        def copy(e, out, in_):
            if e == "S":
                nc.scalar.copy(out=out, in_=in_)
            elif e == "V":
                nc.vector.tensor_copy(out=out, in_=in_)
            else:
                nc.gpsimd.tensor_scalar(out=out, in0=in_, scalar1=1.0, scalar2=1.0, op0=ALU.mult, op1=ALU.mult)

        def load(e, n, h):
            view = src[n].rearrange("(p j) d -> p j d", j=4)
            if h < 0:
                nc.sync.dma_start(out=raw[n][:], in_=view)
            else:
                nc.sync.dma_start(out=raw[n][:, 2 * h : 2 * h + 2, :], in_=view[:, 2 * h : 2 * h + 2, :])

        def turn(e, n, h):
            t = pools["tp"].tile([P, 4, P], F32, name="turned")
            bank[("turn", n, h)] = t
            words = raw[n][:].rearrange("p j d -> p (j d)").bitcast(F32)
            for s in (0, 1):
                for u in (0, 1):
                    w0 = 256 * (2 * h + s)
                    nc.tensor.transpose(t[:, 2 * s + u, :], words[:, w0 + u : w0 + 256 : 2], ident[:])

        def untangle(e, n, h):
            out = flat(n).bitcast(F32)[:, 512 * h : 512 * h + 512].rearrange("p (s m u) -> p s m u", s=2, u=2)
            copy(e, out, bank[("turn", n, h)][:].rearrange("p (s u) m -> p s m u", u=2))

        def il(e, n, t0, t1):
            out = flat(n)[:, 512 * t0 : 512 * t1].rearrange("p (t m j) -> p t m j", t=t1 - t0, j=4)
            copy(e, out, raw[n][:].rearrange("p j (m t) -> p t m j", t=4)[:, t0:t1, :, :])

        def quant(e, n, s0, s1):
            nc.vector.quantize_mx(out=fp8(n, 128 * s0, 128 * s1), scales=scal[n][:, 128 * s0 : 128 * s1], in_=flat(n)[:, 512 * s0 : 512 * s1])

        def proj(e, z, s):
            w, a = OF[z]
            t = pools["s1"].tile([P, 4, P], F32, name="proj")
            bank[("proj", z, s)] = t
            for j in range(4):
                nc.tensor.matmul_mx(out=t[:, j, :], lhsT=fp8(w, 128 * j, 128 * j + 128), lhsT_scale=scal[w][:, 128 * j : 128 * j + 128],
                                    rhs=fp8(a, 128 * s, 128 * s + 128), rhs_scale=scal[a][:, 128 * s : 128 * s + 128], start=True, stop=True)

        def evac(e, z, s):
            copy(e, grp[z][:, 128 * s : 128 * s + 128, :], bank[("proj", z, s)][:].rearrange("p t m -> p m t"))

        def score(e, n, r):
            t = pools["s2"].tile([P, N], F32, name="score")
            bank[("score", n, r)] = t
            for i, (a, c) in enumerate((("r", "t"), ("q%d" % n, "k%d" % n))):
                nc.tensor.matmul_mx(out=t[:], lhsT=fp8(a, 128 * r, 128 * r + 128), lhsT_scale=scal[a][:, 128 * r : 128 * r + 128],
                                    rhs=fp8(c, 0, N), rhs_scale=scal[c][:], start=(i == 0), stop=(i == 1))

        def bias(e, n, r):
            nc.vector.scalar_tensor_tensor(out=logit[n][:, r, :].rearrange("p (m s) -> p m s", s=4), in0=bank[("score", n, r)][:].rearrange("p (s m) -> p m s", s=4),
                                           scalar=1.0 / 32.0, in1=raw["b"][:, r, :].rearrange("p (m s) -> p m s", s=4), op0=ALU.mult, op1=ALU.add)

        def peakf(e, n, r):
            nc.vector.tensor_reduce(out=peak[n][:, r : r + 1], in_=logit[n][:, r, :], axis=AX.X, op=ALU.max, negate=True)

        def expf(e, n, r):
            nc.scalar.activation(out=expo[n][:, r, :], in_=logit[n][:, r, :], func=ACT.Exp, bias=peak[n][:, r : r + 1], scale=1.0, accum_out=tot[n][:, r : r + 1])

        def recip(e, n, r):
            nc.vector.reciprocal(out=inv[n][:, r : r + 1], in_=tot[n][:, r : r + 1])
            if ("S", n, r) in scaled_on:
                nc.vector.tensor_scalar(out=inv[n][:, r : r + 1], in0=inv[n][:, r : r + 1], scalar1=512.0, scalar2=None, op0=ALU.mult)

        def scale(e, n, r):
            if e == "S":
                nc.scalar.activation(out=outf[n][:, r, :], in_=expo[n][:, r, :], func=ACT.Copy, scale=inv[n][:, r : r + 1])
            else:
                eng = nc.vector if e == "V" else nc.gpsimd
                eng.tensor_scalar(out=outf[n][:, r, :], in0=expo[n][:, r, :], scalar1=inv[n][:, r : r + 1], scalar2=512.0, op0=ALU.mult, op1=ALU.mult)
            nc.sync.dma_start(out=out_0[n].rearrange("(p r) k -> p r k", r=4)[:, r, :], in_=outf[n][:, r, :])

        def inter(e, n, c0, c1):
            copy(e, grp["o%d" % n][:, 128 * c0 : 128 * c1, :], outf[n][:].rearrange("p r k -> p k r")[:, 128 * c0 : 128 * c1, :])

        def qout(e, n, c0, c1):
            o = "o%d" % n
            quant("V", o, c0, c1)
            nc.sync.dma_start(out=words_out[:, 2048 * n + 512 * c0 : 2048 * n + 512 * c1].bitcast(I32), in_=codes[o][:, 128 * c0 : 128 * c1].bitcast(I32))
            done.extend([(n, c) for c in range(c0, c1)])
            if all((n, c) in done for c in range(4)):
                for q in range(4):
                    nc.sync.dma_start(out=out_2[0][4 * q : 4 * q + 4, 512 * n : 512 * n + 512].bitcast(I32), in_=scal[o][32 * q : 32 * q + 4, :].bitcast(I32))

        done = []
        scaled_on = [(e, a[0], a[1]) for k, e, a in PLAN if k == "scale"]
        table = {"load": load, "turn": turn, "untangle": untangle, "il": il, "quant": quant, "proj": proj, "evac": evac, "score": score,
                 "bias": bias, "peak": peakf, "exp": expf, "recip": recip, "scale": scale, "inter": inter, "qout": qout}
        with tc.manual_schedule():
            nc.vector.memset(warm[:], 0.0)
            nc.scalar.activation(out=warm[:, 1:2], in_=warm[:, 0:1], func=ACT.Exp)
            make_identity(nc, ident[:])
            for k, e, a in PLAN:
                table[k](e, *a)
